import numpy as np
import ml_dtypes


def mxq(x, axis, fmt="e4m3"):
    dtype, down = {"e4m3": (ml_dtypes.float8_e4m3fn, 7), "e5m2": (ml_dtypes.float8_e5m2, 14)}[fmt]
    v = np.moveaxis(np.asarray(x, np.float32).astype(ml_dtypes.bfloat16).astype(np.float64), axis, -1)
    blocks = v.reshape(v.shape[:-1] + (-1, 32))
    amax = np.abs(blocks).max(-1, keepdims=True)
    byte = np.maximum(np.where(amax > 0, np.frexp(amax)[1] - 1 + 127, 0) - down, 1)
    scale = np.exp2(byte - 127.0)
    codes = (blocks / scale).astype(np.float32).astype(dtype).astype(np.float64)
    return np.moveaxis((codes * scale).reshape(v.shape), -1, axis)


WIDE = False


def mx_kscale(k):
    if not WIDE:
        return np.ones(k)
    levels = np.array([10, -10, 5, -5, 0])
    if k % 512:
        return np.exp2(np.random.permutation(np.resize(levels, k // 32))).repeat(32)
    a = np.empty((k // 512, 16))
    for p in range(k // 512):
        a[p, :8] = np.random.permutation(np.resize(levels, 8))
        for g in range(8):
            far = levels[np.abs(levels - a[p, g]) >= 10]
            a[p, g + 8] = far[np.random.randint(len(far))]
    return np.exp2(a.ravel()).repeat(32)


def f64(x):
    return np.asarray(x).astype(np.float64)


def striped(idx):
    return np.tile(idx.reshape(-1, 16).T, (8, 1)).astype(np.uint16)


def unstriped(offs):
    return offs[:16].T.reshape(-1).astype(np.int64)


def pack_weight(w):
    k, n = w.shape
    w = f64(np.asarray(w, np.float32).astype(ml_dtypes.bfloat16)).reshape(k // 32, 32, n)
    amax = np.abs(w).max(1)
    byte = np.clip(np.where(amax > 0, np.frexp(amax)[1] - 1 + 127 - 7, 1), 1, 254)
    scaled = (w * np.exp2(127.0 - byte)[:, None, :]).reshape(k, n).astype(np.float32)
    words = np.ascontiguousarray(scaled.reshape(k // 512, 128, 4, n).transpose(0, 1, 3, 2)).astype(ml_dtypes.float8_e4m3fn).view(np.uint8)
    return words, np.ascontiguousarray(byte.astype(np.uint8).reshape(k // 512, 16, n))


def unpack_weight(words, scales):
    g, p, n, _ = words.shape
    vals = np.ascontiguousarray(words).view(ml_dtypes.float8_e4m3fn).astype(np.float64) * np.repeat(np.exp2(scales.astype(np.float64) - 127.0), 8, axis=1)[..., None]
    return vals.transpose(0, 1, 3, 2).reshape(g * 512, n)


def gelu(v):
    return 0.5 * v * (1.0 + np.tanh(np.sqrt(2.0 / np.pi) * (v + 0.044715 * v**3)))


K, T, S, H, V, Z, W = 512, 2048, 512, 512, 256, 512, 2048
P = 2 ** 7


def setup_inputs():
    n = np.random.standard_normal
    s = mx_kscale(K)[:, None]
    packed_xT = pack_weight(n((K, T)) * s)
    packed_eT = pack_weight(n((K, W)) * s)
    return {
        "x_words": packed_xT[0],
        "x_scales": packed_xT[1],
        "w1": (n((K, H)) / np.sqrt(K) / s).astype(np.float32),
        "sc_": (np.random.uniform(0.5, 1.5, (H, V))).astype(np.float32),
        "e_words": packed_eT[0],
        "e_scales": packed_eT[1],
        "unit": (np.random.uniform(0.6, 1.4, (K, 1)) / np.sqrt(K) / s).astype(np.float32),
        "lat": (np.tile(np.random.uniform(-1.0, 1.0, W), (P, 1))).astype(np.float32),
        "offs": striped(np.random.permutation(T)[:S]),
        "nb": striped(np.random.permutation(S)),
        "pk": striped(np.random.permutation(S)[:V]),
        "cell": striped(np.random.permutation(W)[:Z]),
    }


def reference(x_words, x_scales, w1, sc_, e_words, e_scales, unit, lat, offs, nb, pk, cell):
    xq = unpack_weight(x_words, x_scales)[:, unstriped(offs)]
    y = mxq(f64(w1), 0, "e4m3").T @ xq
    yn = y[:, unstriped(nb)]
    cont = y - (0.7 * yn)
    act_ = gelu(cont)
    apk = act_[:, unstriped(pk)]
    emb = apk * f64(sc_)
    hid = f64(unit) * emb
    e_cell = unpack_weight(e_words, e_scales)[:, unstriped(cell)]
    sc = mxq(hid, 0, "e4m3").T @ e_cell
    es = np.exp(1.3 * np.tanh(sc))
    el = es * (f64(lat)[:1][:, unstriped(cell)])
    num = el.sum(axis=1, keepdims=True)
    den = es.sum(axis=1, keepdims=True)
    mlat = num / den
    dl = f64(lat)[:1][:, unstriped(cell)] - mlat
    dl2 = (dl) ** 2
    return es * (dl2 / (dl2 + 0.5))

@@ -1,0 +1,212 @@
+from contextlib import ExitStack
+
+import concourse.mybir as mybir
+
+K, T, S, H, V, Z, W = 512, 2048, 512, 512, 256, 512, 2048
+FLOPS = 2 * K * H * S + 2 * H * V * Z
+
+F32 = mybir.dt.float32
+BF16 = mybir.dt.bfloat16
+I32 = mybir.dt.int32
+U32 = mybir.dt.uint32
+U16 = mybir.dt.uint16
+U8 = mybir.dt.uint8
+FP8X4 = mybir.dt.float8_e4m3fn_x4
+ALU = mybir.AluOpType
+ACT = mybir.ActivationFunctionType
+
+P = 128
+PACK = 4
+QUAD = 32
+Y_WINDOW = 704
+W_SPLIT = 48
+
+
+def tile_picked_ygeolok_dev_p_kernel(tc, x_words, x_scales, w1, sc_, e_words, e_scales, unit, lat, offs, nb, pk, cell, out):
+    nc = tc.nc
+    with ExitStack() as ctx:
+        keep = ctx.enter_context(tc.tile_pool(name="keep", bufs=1))
+        psum = ctx.enter_context(tc.psum_pool(name="psum", bufs=1))
+
+        def sb(name, shape, dtype):
+            return keep.tile(shape, dtype, name=name, align_bytes=64)
+
+        offs_t = sb("offs_t", [P, S // 16], U16)
+        nb_t = sb("nb_t", [P, S // 16], U16)
+        pk_t = sb("pk_t", [P, V // 16], U16)
+        cell_t = sb("cell_t", [P, Z // 16], U16)
+        xw_tab = sb("xw_tab", [P, T], U32)
+        xs_tab = sb("xs_tab", [P, T], U8)
+        ew_tab = sb("ew_tab", [P, W], U32)
+        es_tab = sb("es_tab", [P, W], U8)
+        lat_tab = sb("lat_tab", [P, W], F32)
+        w_raw = sb("w_raw", [P, PACK, H], F32)
+        sc_t = sb("sc_t", [P, PACK, V], F32)
+        unit_t = sb("unit_t", [P, PACK], F32)
+        y = [sb(f"y{t}", [P, Y_WINDOW], F32) for t in range(PACK)]
+
+        def load_scales(queue, table, rows):
+            for q in range(P // QUAD):
+                queue.dma_start(out=table[QUAD * q : QUAD * q + 4, :].bitcast(I32), in_=rows[0, 4 * q : 4 * q + 4, :].bitcast(I32))
+
+        def load_words(table, words):
+            nc.sync.dma_start(out=table[:].bitcast(I32), in_=words[0].rearrange("p n t -> p (n t)").bitcast(I32))
+
+        nc.gpsimd.memset(xs_tab[:].bitcast(I32), 0)
+        nc.gpsimd.memset(es_tab[:].bitcast(I32), 0)
+        for t in range(PACK):
+            nc.gpsimd.memset(y[t][:, S:], 0.0)
+
+        nc.sync.dma_start(out=w_raw[:], in_=w1.rearrange("(p j) c -> p j c", j=PACK))
+        nc.sync.dma_start(offs_t[:], offs)
+        load_scales(nc.scalar, xs_tab, x_scales)
+        load_words(xw_tab, x_words)
+        nc.sync.dma_start(cell_t[:], cell)
+        load_scales(nc.sync, es_tab, e_scales)
+        nc.sync.dma_start(nb_t[:], nb)
+        nc.sync.dma_start(out=sc_t[:], in_=sc_.rearrange("(p t) v -> p t v", t=PACK))
+        nc.sync.dma_start(out=unit_t[:], in_=unit.rearrange("(p t) o -> p (t o)", t=PACK))
+        load_words(ew_tab, e_words)
+        nc.sync.dma_start(pk_t[:], pk)
+        nc.sync.dma_start(out=lat_tab[:], in_=lat)
+
+        w_bf = sb("w_bf", [P, PACK, P, PACK], BF16)
+        w_dst = w_bf[:].rearrange("p t m j -> p m t j")
+        w_src = w_raw[:].rearrange("p j (m t) -> p m t j", t=PACK)
+        xs = sb("xs", [P, S], U8)
+        xw = sb("xw", [P, S], U32)
+        es_b = sb("es_b", [P, Z], U8)
+        nc.vector.tensor_copy(xs[:], xs_tab[:].indirect(offs_t[:]))
+        nc.scalar.copy(w_dst[:, :W_SPLIT], w_src[:, :W_SPLIT])
+        nc.vector.tensor_copy(w_dst[:, W_SPLIT:], w_src[:, W_SPLIT:])
+        w_codes = sb("w_codes", [P, H], U32)
+        w_scales = sb("w_scales", [P, H], U8)
+        nc.vector.quantize_mx(out=w_codes[:].bitcast(FP8X4), scales=w_scales[:], in_=w_bf[:].rearrange("p t m j -> p (t m j)"))
+        nc.vector.tensor_copy(xw[:], xw_tab[:].indirect(offs_t[:]))
+
+        y_ps = [psum.tile([P, S], F32, name=f"y_ps{t}") for t in range(PACK)]
+        for t in range(PACK):
+            cols = slice(t * P, (t + 1) * P)
+            nc.tensor.matmul_mx(out=y_ps[t][:], lhsT=w_codes[:, cols].bitcast(FP8X4), lhsT_scale=w_scales[:, cols],
+                                rhs=xw[:].bitcast(FP8X4), rhs_scale=xs[:], start=True, stop=True)
+
+        factor = sb("factor", [P, V, PACK], F32)
+
+        def factors(h):
+            cols = slice(h * P, (h + 1) * P)
+            nc.vector.tensor_tensor(factor[:, cols, :], sc_t[:, :, cols].rearrange("p t v -> p v t"),
+                                    unit_t[:].unsqueeze(1).to_broadcast([P, P, PACK]), ALU.mult)
+
+        ew = sb("ew", [P, Z], U32)
+        yn = [sb(f"yn{t}", [P, S], F32) for t in range(PACK)]
+        cont = [sb(f"cont{t}", [P, S], F32) for t in range(PACK)]
+        cpk = [sb(f"cpk{h}", [P, PACK, P], F32) for h in range(2)]
+        apk = [sb(f"apk{h}", [P, P, PACK], F32) for h in range(2)]
+        hid = [sb(f"hid{h}", [P, P, PACK], BF16) for h in range(2)]
+        h_codes = [sb(f"h_codes{h}", [P, P], U32) for h in range(2)]
+        h_scales = [sb(f"h_scales{h}", [P, P], U8) for h in range(2)]
+        sc_ps = [psum.tile([P, Z], F32, name=f"sc_ps{h}") for h in range(2)]
+        halves = [slice(h * P, (h + 1) * P) for h in range(2)]
+
+        def gather(dst, window, on_vector):
+            if on_vector:
+                nc.vector.tensor_copy(dst, window)
+            else:
+                nc.scalar.activation(dst, window, ACT.Copy)
+
+        def copy_y(t, on_vector):
+            if on_vector:
+                nc.vector.tensor_copy(y[t][:, :S], y_ps[t][:])
+            else:
+                nc.scalar.copy(y[t][:, :S], y_ps[t][:])
+
+        def neighbours(t, on_vector):
+            gather(yn[t][:], y[t][:].indirect(nb_t[:]), on_vector)
+
+        def contrast(t):
+            nc.vector.scalar_tensor_tensor(cont[t][:], yn[t][:], -0.7, y_ps[t][:], ALU.mult, ALU.add)
+
+        def crops(h, t, on_vector):
+            gather(cpk[h][:, t, :], cont[t][:].indirect(pk_t[:, h * (P // 16) : (h + 1) * (P // 16)]), on_vector)
+
+        def rectify(h):
+            nc.scalar.activation(apk[h][:], cpk[h][:].rearrange("p t v -> p v t"), ACT.Gelu_apprx_tanh)
+
+        def hidden(h):
+            nc.vector.tensor_tensor(hid[h][:], apk[h][:], factor[:, halves[h], :], ALU.mult)
+
+        def scores(h):
+            nc.vector.quantize_mx(out=h_codes[h][:].bitcast(FP8X4), scales=h_scales[h][:], in_=hid[h][:].rearrange("p v t -> p (v t)"))
+            nc.tensor.matmul_mx(out=sc_ps[h][:], lhsT=h_codes[h][:].bitcast(FP8X4), lhsT_scale=h_scales[h][:],
+                                rhs=ew[:].bitcast(FP8X4), rhs_scale=es_b[:], start=True, stop=True)
+
+        nc.vector.tensor_copy(es_b[:], es_tab[:].indirect(cell_t[:]))
+        factors(0)
+        copy_y(0, False)
+        copy_y(1, False)
+        neighbours(0, True)
+        copy_y(2, False)
+        copy_y(3, False)
+        neighbours(1, True)
+        neighbours(2, False)
+        contrast(0)
+        contrast(1)
+        neighbours(3, False)
+        contrast(2)
+        crops(0, 0, False)
+        contrast(3)
+        crops(0, 1, False)
+        crops(0, 2, False)
+        crops(1, 0, True)
+        crops(0, 3, False)
+        crops(1, 1, True)
+        crops(1, 2, True)
+        rectify(0)
+        nc.vector.tensor_copy(ew[:], ew_tab[:].indirect(cell_t[:]))
+        crops(1, 3, False)
+        rectify(1)
+        hidden(0)
+        factors(1)
+        scores(0)
+        hidden(1)
+        scores(1)
+
+
+        lat_c = sb("lat_c", [P, Z], F32)
+        nc.vector.tensor_copy(lat_c[:], lat_tab[:].indirect(cell_t[:]))
+
+        def pair(name, width):
+            return [sb(f"{name}{h}", [P, width], F32) for h in range(2)]
+
+        th, es, el, d2, q, rec, wgt, res = (pair(n, Z) for n in ("th", "es", "el", "d2", "q", "rec", "wgt", "res"))
+        dl = sb("dl", [P, Z], F32)
+        den, num, rden, rden2 = (pair(n, 1) for n in ("den", "num", "rden", "rden2"))
+        for h in range(2):
+            nc.scalar.activation(th[h][:], sc_ps[h][:], ACT.Tanh)
+            nc.scalar.activation(es[h][:], th[h][:], ACT.Exp, scale=1.3, accum_out=den[h][:])
+
+        def numerator(h):
+            nc.vector.scalar_tensor_tensor(el[h][:], es[h][:], -1.0, lat_c[:], ALU.mult, ALU.mult, accum_out=num[h][:])
+
+        numerator(0)
+        nc.vector.reciprocal(rden[0][:], den[0][:])
+        nc.vector.tensor_scalar(dl[:], lat_c[:], den[0][:], num[0][:], ALU.mult, ALU.add)
+        nc.vector.tensor_tensor(rden2[0][:], rden[0][:], rden[0][:], ALU.mult)
+        numerator(1)
+        nc.vector.scalar_tensor_tensor(d2[0][:], dl[:], rden2[0][:], dl[:], ALU.mult, ALU.mult)
+        nc.scalar.activation(rden[1][:], den[1][:], ACT.Abs_reciprocal_sqrt, scale=den[1][:])
+        nc.scalar.activation(d2[1][:], lat_c[:], ACT.Square, scale=den[1][:], bias=num[1][:])
+        nc.vector.tensor_tensor(rden2[1][:], rden[1][:], rden[1][:], ALU.mult)
+        nc.vector.scalar_tensor_tensor(q[0][:], d2[0][:], 1.0, d2[0][:], ALU.add, ALU.mult)
+        nc.scalar.activation(q[1][:], d2[1][:], ACT.Square, scale=rden2[1][:], bias=0.5)
+        nc.vector.tensor_tensor(wgt[0][:], d2[0][:], es[0][:], ALU.mult)
+        nc.scalar.activation(rec[0][:], q[0][:], ACT.Abs_reciprocal_sqrt, bias=0.25)
+        nc.vector.scalar_tensor_tensor(wgt[1][:], d2[1][:], rden2[1][:], es[1][:], ALU.mult, ALU.mult)
+        cells = [slice(0, Z // 2), slice(Z // 2, Z)]
+        for c in cells:
+            nc.scalar.activation(rec[1][:, c], q[1][:, c], ACT.Abs_reciprocal_sqrt)
+        nc.vector.tensor_tensor(res[0][:], wgt[0][:], rec[0][:], ALU.mult)
+        nc.sync.dma_start(out=out[halves[0], :], in_=res[0][:])
+        for c in cells:
+            nc.vector.tensor_tensor(res[1][:, c], wgt[1][:, c], rec[1][:, c], ALU.mult)
+            nc.sync.dma_start(out=out[halves[1], c], in_=res[1][:, c])

@@ -19,7 +19,7 @@ P = 128
 PACK = 4
 QUAD = 32
 Y_WINDOW = 704
-W_SPLIT = 48
+W_SPLIT = 96
 
 
 def tile_picked_ygeolok_dev_p_kernel(tc, x_words, x_scales, w1, sc_, e_words, e_scales, unit, lat, offs, nb, pk, cell, out):
@@ -28,8 +28,8 @@ def tile_picked_ygeolok_dev_p_kernel(tc, x_words, x_scales, w1, sc_, e_words, e_
         keep = ctx.enter_context(tc.tile_pool(name="keep", bufs=1))
         psum = ctx.enter_context(tc.psum_pool(name="psum", bufs=1))
 
-        def sb(name, shape, dtype):
-            return keep.tile(shape, dtype, name=name, align_bytes=64)
+        def sb(name, shape, dtype, tag=None):
+            return keep.tile(shape, dtype, name=name, tag=tag or name, align_bytes=64)
 
         offs_t = sb("offs_t", [P, S // 16], U16)
         nb_t = sb("nb_t", [P, S // 16], U16)
@@ -45,24 +45,27 @@ def tile_picked_ygeolok_dev_p_kernel(tc, x_words, x_scales, w1, sc_, e_words, e_
         unit_t = sb("unit_t", [P, PACK], F32)
         y = [sb(f"y{t}", [P, Y_WINDOW], F32) for t in range(PACK)]
 
-        def load_scales(queue, table, rows):
-            for q in range(P // QUAD):
+        def load_scales(queues, table, rows):
+            for q, queue in enumerate(queues):
                 queue.dma_start(out=table[QUAD * q : QUAD * q + 4, :].bitcast(I32), in_=rows[0, 4 * q : 4 * q + 4, :].bitcast(I32))
 
         def load_words(table, words):
             nc.sync.dma_start(out=table[:].bitcast(I32), in_=words[0].rearrange("p n t -> p (n t)").bitcast(I32))
 
         nc.gpsimd.memset(xs_tab[:].bitcast(I32), 0)
+        warm = sb("warm", [P, 3], F32)
+        nc.gpsimd.memset(warm[:, 0:1], 0.0)
         nc.gpsimd.memset(es_tab[:].bitcast(I32), 0)
         for t in range(PACK):
             nc.gpsimd.memset(y[t][:, S:], 0.0)
 
         nc.sync.dma_start(out=w_raw[:], in_=w1.rearrange("(p j) c -> p j c", j=PACK))
         nc.sync.dma_start(offs_t[:], offs)
-        load_scales(nc.scalar, xs_tab, x_scales)
+        load_scales((nc.scalar, nc.scalar, nc.sync, nc.sync), xs_tab, x_scales)
+        nc.scalar.activation(warm[:, 1:2], warm[:, 0:1], ACT.Gelu_apprx_tanh)
         load_words(xw_tab, x_words)
         nc.sync.dma_start(cell_t[:], cell)
-        load_scales(nc.sync, es_tab, e_scales)
+        load_scales((nc.sync,) * 4, es_tab, e_scales)
         nc.sync.dma_start(nb_t[:], nb)
         nc.sync.dma_start(out=sc_t[:], in_=sc_.rearrange("(p t) v -> p t v", t=PACK))
         nc.sync.dma_start(out=unit_t[:], in_=unit.rearrange("(p t) o -> p (t o)", t=PACK))
@@ -75,10 +78,10 @@ def tile_picked_ygeolok_dev_p_kernel(tc, x_words, x_scales, w1, sc_, e_words, e_
         w_src = w_raw[:].rearrange("p j (m t) -> p m t j", t=PACK)
         xs = sb("xs", [P, S], U8)
         xw = sb("xw", [P, S], U32)
-        es_b = sb("es_b", [P, Z], U8)
-        nc.vector.tensor_copy(xs[:], xs_tab[:].indirect(offs_t[:]))
+        es_b = sb("es_b", [P, Z], U8, tag="xw_tab")
         nc.scalar.copy(w_dst[:, :W_SPLIT], w_src[:, :W_SPLIT])
         nc.vector.tensor_copy(w_dst[:, W_SPLIT:], w_src[:, W_SPLIT:])
+        nc.vector.tensor_copy(xs[:], xs_tab[:].indirect(offs_t[:]))
         w_codes = sb("w_codes", [P, H], U32)
         w_scales = sb("w_scales", [P, H], U8)
         nc.vector.quantize_mx(out=w_codes[:].bitcast(FP8X4), scales=w_scales[:], in_=w_bf[:].rearrange("p t m j -> p (t m j)"))
@@ -90,14 +93,14 @@ def tile_picked_ygeolok_dev_p_kernel(tc, x_words, x_scales, w1, sc_, e_words, e_
             nc.tensor.matmul_mx(out=y_ps[t][:], lhsT=w_codes[:, cols].bitcast(FP8X4), lhsT_scale=w_scales[:, cols],
                                 rhs=xw[:].bitcast(FP8X4), rhs_scale=xs[:], start=True, stop=True)
 
-        factor = sb("factor", [P, V, PACK], F32)
+        factor = [sb(f"factor{h}", [P, P, PACK], F32, tag=tag) for h, tag in enumerate(("es_tab", "apk0"))]
 
         def factors(h):
             cols = slice(h * P, (h + 1) * P)
-            nc.vector.tensor_tensor(factor[:, cols, :], sc_t[:, :, cols].rearrange("p t v -> p v t"),
+            nc.vector.tensor_tensor(factor[h][:], sc_t[:, :, cols].rearrange("p t v -> p v t"),
                                     unit_t[:].unsqueeze(1).to_broadcast([P, P, PACK]), ALU.mult)
 
-        ew = sb("ew", [P, Z], U32)
+        ew = sb("ew", [P, Z], U32, tag="yn3")
         yn = [sb(f"yn{t}", [P, S], F32) for t in range(PACK)]
         cont = [sb(f"cont{t}", [P, S], F32) for t in range(PACK)]
         cpk = [sb(f"cpk{h}", [P, PACK, P], F32) for h in range(2)]
@@ -133,7 +136,7 @@ def tile_picked_ygeolok_dev_p_kernel(tc, x_words, x_scales, w1, sc_, e_words, e_
             nc.scalar.activation(apk[h][:], cpk[h][:].rearrange("p t v -> p v t"), ACT.Gelu_apprx_tanh)
 
         def hidden(h):
-            nc.vector.tensor_tensor(hid[h][:], apk[h][:], factor[:, halves[h], :], ALU.mult)
+            nc.vector.tensor_tensor(hid[h][:], apk[h][:], factor[h][:], ALU.mult)
 
         def scores(h):
             nc.vector.quantize_mx(out=h_codes[h][:].bitcast(FP8X4), scales=h_scales[h][:], in_=hid[h][:].rearrange("p v t -> p (v t)"))
@@ -158,11 +161,11 @@ def tile_picked_ygeolok_dev_p_kernel(tc, x_words, x_scales, w1, sc_, e_words, e_
         crops(0, 1, False)
         crops(0, 2, False)
         crops(1, 0, True)
-        crops(0, 3, False)
         crops(1, 1, True)
-        crops(1, 2, True)
-        rectify(0)
+        crops(0, 3, False)
         nc.vector.tensor_copy(ew[:], ew_tab[:].indirect(cell_t[:]))
+        rectify(0)
+        crops(1, 2, False)
         crops(1, 3, False)
         rectify(1)
         hidden(0)
@@ -172,7 +175,8 @@ def tile_picked_ygeolok_dev_p_kernel(tc, x_words, x_scales, w1, sc_, e_words, e_
         scores(1)
 
 
-        lat_c = sb("lat_c", [P, Z], F32)
+        nc.scalar.activation(warm[:, 2:3], apk[1][:, 0, 0:1], ACT.Exp)
+        lat_c = sb("lat_c", [P, Z], F32, tag="hid1")
         nc.vector.tensor_copy(lat_c[:], lat_tab[:].indirect(cell_t[:]))
 
         def pair(name, width):

@@ -19,7 +19,7 @@ P = 128
 PACK = 4
 QUAD = 32
 Y_WINDOW = 704
-W_SPLIT = 96
+W_SPLIT = 80
 
 
 def tile_picked_ygeolok_dev_p_kernel(tc, x_words, x_scales, w1, sc_, e_words, e_scales, unit, lat, offs, nb, pk, cell, out):
@@ -74,15 +74,15 @@ def tile_picked_ygeolok_dev_p_kernel(tc, x_words, x_scales, w1, sc_, e_words, e_
         nc.sync.dma_start(out=lat_tab[:], in_=lat)
 
         w_bf = sb("w_bf", [P, PACK, P, PACK], BF16)
-        w_dst = w_bf[:].rearrange("p t m j -> p m t j")
-        w_src = w_raw[:].rearrange("p j (m t) -> p m t j", t=PACK)
+        w_dst = w_bf[:].rearrange("p t m j -> p m j t")
+        w_src = w_raw[:].rearrange("p j (m t) -> p m j t", t=PACK)
         xs = sb("xs", [P, S], U8)
         xw = sb("xw", [P, S], U32)
         es_b = sb("es_b", [P, Z], U8, tag="xw_tab")
         nc.scalar.copy(w_dst[:, :W_SPLIT], w_src[:, :W_SPLIT])
         nc.vector.tensor_copy(w_dst[:, W_SPLIT:], w_src[:, W_SPLIT:])
         nc.vector.tensor_copy(xs[:], xs_tab[:].indirect(offs_t[:]))
-        w_codes = sb("w_codes", [P, H], U32)
+        w_codes = sb("w_codes", [P, H], U32, tag="xs_tab")
         w_scales = sb("w_scales", [P, H], U8)
         nc.vector.quantize_mx(out=w_codes[:].bitcast(FP8X4), scales=w_scales[:], in_=w_bf[:].rearrange("p t m j -> p (t m j)"))
         nc.vector.tensor_copy(xw[:], xw_tab[:].indirect(offs_t[:]))
@@ -93,16 +93,16 @@ def tile_picked_ygeolok_dev_p_kernel(tc, x_words, x_scales, w1, sc_, e_words, e_
             nc.tensor.matmul_mx(out=y_ps[t][:], lhsT=w_codes[:, cols].bitcast(FP8X4), lhsT_scale=w_scales[:, cols],
                                 rhs=xw[:].bitcast(FP8X4), rhs_scale=xs[:], start=True, stop=True)
 
-        factor = [sb(f"factor{h}", [P, P, PACK], F32, tag=tag) for h, tag in enumerate(("es_tab", "apk0"))]
+        factor = [sb(f"factor{h}", [P, P, PACK], F32) for h in range(2)]
 
         def factors(h):
             cols = slice(h * P, (h + 1) * P)
-            nc.vector.tensor_tensor(factor[h][:], sc_t[:, :, cols].rearrange("p t v -> p v t"),
+            nc.gpsimd.tensor_tensor(factor[h][:], sc_t[:, :, cols].rearrange("p t v -> p v t"),
                                     unit_t[:].unsqueeze(1).to_broadcast([P, P, PACK]), ALU.mult)
 
         ew = sb("ew", [P, Z], U32, tag="yn3")
         yn = [sb(f"yn{t}", [P, S], F32) for t in range(PACK)]
-        cont = [sb(f"cont{t}", [P, S], F32) for t in range(PACK)]
+        cont = [sb(f"cont{t}", [P, S], F32, tag="sc_t" if t == 2 else None) for t in range(PACK)]
         cpk = [sb(f"cpk{h}", [P, PACK, P], F32) for h in range(2)]
         apk = [sb(f"apk{h}", [P, P, PACK], F32) for h in range(2)]
         hid = [sb(f"hid{h}", [P, P, PACK], BF16) for h in range(2)]
@@ -126,6 +126,9 @@ def tile_picked_ygeolok_dev_p_kernel(tc, x_words, x_scales, w1, sc_, e_words, e_
         def neighbours(t, on_vector):
             gather(yn[t][:], y[t][:].indirect(nb_t[:]), on_vector)
 
+        def contrast_on_gpsimd(t):
+            nc.gpsimd.tensor_tensor(cont[t][:], yn[t][:], y[t][:, :S], ALU.add)
+
         def contrast(t):
             nc.vector.scalar_tensor_tensor(cont[t][:], yn[t][:], -0.7, y_ps[t][:], ALU.mult, ALU.add)
 
@@ -133,7 +136,7 @@ def tile_picked_ygeolok_dev_p_kernel(tc, x_words, x_scales, w1, sc_, e_words, e_
             gather(cpk[h][:, t, :], cont[t][:].indirect(pk_t[:, h * (P // 16) : (h + 1) * (P // 16)]), on_vector)
 
         def rectify(h):
-            nc.scalar.activation(apk[h][:], cpk[h][:].rearrange("p t v -> p v t"), ACT.Gelu_apprx_tanh)
+            nc.scalar.activation(apk[h][:].rearrange("p (c i) t -> p c t i", i=4), cpk[h][:].rearrange("p t (c i) -> p c t i", i=4), ACT.Gelu_apprx_tanh)
 
         def hidden(h):
             nc.vector.tensor_tensor(hid[h][:], apk[h][:], factor[h][:], ALU.mult)
@@ -145,31 +148,31 @@ def tile_picked_ygeolok_dev_p_kernel(tc, x_words, x_scales, w1, sc_, e_words, e_
 
         nc.vector.tensor_copy(es_b[:], es_tab[:].indirect(cell_t[:]))
         factors(0)
+        factors(1)
         copy_y(0, False)
         copy_y(1, False)
         neighbours(0, True)
         copy_y(2, False)
         copy_y(3, False)
         neighbours(1, True)
-        neighbours(2, False)
+        nc.scalar.activation(yn[2][:], y[2][:].indirect(nb_t[:]), ACT.Copy, scale=-0.7)
         contrast(0)
+        contrast_on_gpsimd(2)
         contrast(1)
         neighbours(3, False)
-        contrast(2)
-        crops(0, 0, False)
+        crops(0, 0, True)
+        crops(1, 0, True)
         contrast(3)
         crops(0, 1, False)
-        crops(0, 2, False)
-        crops(1, 0, True)
-        crops(1, 1, True)
-        crops(0, 3, False)
-        nc.vector.tensor_copy(ew[:], ew_tab[:].indirect(cell_t[:]))
-        rectify(0)
+        crops(1, 1, False)
+        crops(0, 2, True)
         crops(1, 2, False)
+        crops(0, 3, True)
+        nc.vector.tensor_copy(ew[:], ew_tab[:].indirect(cell_t[:]))
         crops(1, 3, False)
+        rectify(0)
         rectify(1)
         hidden(0)
-        factors(1)
         scores(0)
         hidden(1)
         scores(1)

@@ -78,20 +78,29 @@ def tile_picked_ygeolok_dev_p_kernel(tc, x_words, x_scales, w1, sc_, e_words, e_
         w_src = w_raw[:].rearrange("p j (m t) -> p m j t", t=PACK)
         xs = sb("xs", [P, S], U8)
         xw = sb("xw", [P, S], U32)
-        es_b = sb("es_b", [P, Z], U8, tag="xw_tab")
+        es_b = sb("es_b", [P, Z], U8, tag="w_bf")
         nc.scalar.copy(w_dst[:, :W_SPLIT], w_src[:, :W_SPLIT])
         nc.vector.tensor_copy(w_dst[:, W_SPLIT:], w_src[:, W_SPLIT:])
         nc.vector.tensor_copy(xs[:], xs_tab[:].indirect(offs_t[:]))
-        w_codes = sb("w_codes", [P, H], U32, tag="xs_tab")
-        w_scales = sb("w_scales", [P, H], U8)
-        nc.vector.quantize_mx(out=w_codes[:].bitcast(FP8X4), scales=w_scales[:], in_=w_bf[:].rearrange("p t m j -> p (t m j)"))
-        nc.vector.tensor_copy(xw[:], xw_tab[:].indirect(offs_t[:]))
+        w_codes = [sb(f"w_codes{u}", [P, H // 2], U32, tag=tag) for u, tag in enumerate(("xs_tab", "xw_tab"))]
+        w_scales = [sb(f"w_scales{u}", [P, H // 2], U8) for u in range(2)]
+
+        def quantise_w(u):
+            nc.vector.quantize_mx(out=w_codes[u][:].bitcast(FP8X4), scales=w_scales[u][:], in_=w_bf[:, 2 * u : 2 * u + 2].rearrange("p t m j -> p (t m j)"))
+
+        quantise_w(0)
+        for g in range(2):
+            nc.vector.tensor_copy(xw[:, g * (S // 2) : (g + 1) * (S // 2)], xw_tab[:].indirect(offs_t[:, g * (S // 32) : (g + 1) * (S // 32)]))
+        quantise_w(1)
 
         y_ps = [psum.tile([P, S], F32, name=f"y_ps{t}") for t in range(PACK)]
-        for t in range(PACK):
-            cols = slice(t * P, (t + 1) * P)
-            nc.tensor.matmul_mx(out=y_ps[t][:], lhsT=w_codes[:, cols].bitcast(FP8X4), lhsT_scale=w_scales[:, cols],
-                                rhs=xw[:].bitcast(FP8X4), rhs_scale=xs[:], start=True, stop=True)
+        for u in range(2):
+            for g in range(2):
+                patches = slice(g * (S // 2), (g + 1) * (S // 2))
+                for t in (2 * u, 2 * u + 1):
+                    cols = slice((t % 2) * P, (t % 2 + 1) * P)
+                    nc.tensor.matmul_mx(out=y_ps[t][:, patches], lhsT=w_codes[u][:, cols].bitcast(FP8X4), lhsT_scale=w_scales[u][:, cols],
+                                        rhs=xw[:, patches].bitcast(FP8X4), rhs_scale=xs[:, patches], start=True, stop=True)
 
         factor = [sb(f"factor{h}", [P, P, PACK], F32) for h in range(2)]
 
@@ -100,7 +109,7 @@ def tile_picked_ygeolok_dev_p_kernel(tc, x_words, x_scales, w1, sc_, e_words, e_
             nc.gpsimd.tensor_tensor(factor[h][:], sc_t[:, :, cols].rearrange("p t v -> p v t"),
                                     unit_t[:].unsqueeze(1).to_broadcast([P, P, PACK]), ALU.mult)
 
-        ew = sb("ew", [P, Z], U32, tag="yn3")
+        ew = sb("ew", [P, Z], U32, tag="cont3")
         yn = [sb(f"yn{t}", [P, S], F32) for t in range(PACK)]
         cont = [sb(f"cont{t}", [P, S], F32, tag="sc_t" if t == 2 else None) for t in range(PACK)]
         cpk = [sb(f"cpk{h}", [P, PACK, P], F32) for h in range(2)]
@@ -165,11 +174,11 @@ def tile_picked_ygeolok_dev_p_kernel(tc, x_words, x_scales, w1, sc_, e_words, e_
         contrast(3)
         crops(0, 1, False)
         crops(1, 1, False)
-        crops(0, 2, True)
-        crops(1, 2, False)
+        crops(0, 2, False)
         crops(0, 3, True)
+        crops(1, 2, False)
+        crops(1, 3, True)
         nc.vector.tensor_copy(ew[:], ew_tab[:].indirect(cell_t[:]))
-        crops(1, 3, False)
         rectify(0)
         rectify(1)
         hidden(0)
@@ -197,23 +206,20 @@ def tile_picked_ygeolok_dev_p_kernel(tc, x_words, x_scales, w1, sc_, e_words, e_
 
         numerator(0)
         nc.vector.reciprocal(rden[0][:], den[0][:])
+        numerator(1)
         nc.vector.tensor_scalar(dl[:], lat_c[:], den[0][:], num[0][:], ALU.mult, ALU.add)
         nc.vector.tensor_tensor(rden2[0][:], rden[0][:], rden[0][:], ALU.mult)
-        numerator(1)
         nc.vector.scalar_tensor_tensor(d2[0][:], dl[:], rden2[0][:], dl[:], ALU.mult, ALU.mult)
         nc.scalar.activation(rden[1][:], den[1][:], ACT.Abs_reciprocal_sqrt, scale=den[1][:])
         nc.scalar.activation(d2[1][:], lat_c[:], ACT.Square, scale=den[1][:], bias=num[1][:])
         nc.vector.tensor_tensor(rden2[1][:], rden[1][:], rden[1][:], ALU.mult)
         nc.vector.scalar_tensor_tensor(q[0][:], d2[0][:], 1.0, d2[0][:], ALU.add, ALU.mult)
         nc.scalar.activation(q[1][:], d2[1][:], ACT.Square, scale=rden2[1][:], bias=0.5)
-        nc.vector.tensor_tensor(wgt[0][:], d2[0][:], es[0][:], ALU.mult)
-        nc.scalar.activation(rec[0][:], q[0][:], ACT.Abs_reciprocal_sqrt, bias=0.25)
+        nc.gpsimd.tensor_tensor(wgt[0][:], d2[0][:], es[0][:], ALU.mult)
         nc.vector.scalar_tensor_tensor(wgt[1][:], d2[1][:], rden2[1][:], es[1][:], ALU.mult, ALU.mult)
         cells = [slice(0, Z // 2), slice(Z // 2, Z)]
-        for c in cells:
-            nc.scalar.activation(rec[1][:, c], q[1][:, c], ACT.Abs_reciprocal_sqrt)
-        nc.vector.tensor_tensor(res[0][:], wgt[0][:], rec[0][:], ALU.mult)
-        nc.sync.dma_start(out=out[halves[0], :], in_=res[0][:])
-        for c in cells:
-            nc.vector.tensor_tensor(res[1][:, c], wgt[1][:, c], rec[1][:, c], ALU.mult)
-            nc.sync.dma_start(out=out[halves[1], c], in_=res[1][:, c])
+        for h, bias in enumerate((0.25, 0.0)):
+            for c in cells:
+                nc.scalar.activation(rec[h][:, c], q[h][:, c], ACT.Abs_reciprocal_sqrt, bias=bias)
+                nc.vector.tensor_tensor(res[h][:, c], wgt[h][:, c], rec[h][:, c], ALU.mult)
+                nc.sync.dma_start(out=out[halves[h], c], in_=res[h][:, c])

@@ -18,8 +18,10 @@ ACT = mybir.ActivationFunctionType
 P = 128
 PACK = 4
 QUAD = 32
+LIST_COLUMN = 16
+LINE = 4
 Y_WINDOW = 704
-W_SPLIT = 80
+W_GROUPS_ON_SCALAR = 80
 
 
 def tile_picked_ygeolok_dev_p_kernel(tc, x_words, x_scales, w1, sc_, e_words, e_scales, unit, lat, offs, nb, pk, cell, out):
@@ -28,22 +30,35 @@ def tile_picked_ygeolok_dev_p_kernel(tc, x_words, x_scales, w1, sc_, e_words, e_
         keep = ctx.enter_context(tc.tile_pool(name="keep", bufs=1))
         psum = ctx.enter_context(tc.psum_pool(name="psum", bufs=1))
 
-        def sb(name, shape, dtype, tag=None):
-            return keep.tile(shape, dtype, name=name, tag=tag or name, align_bytes=64)
+        def sb(name, shape, dtype, reuse=None):
+            return keep.tile(shape, dtype, name=name, tag=reuse or name, align_bytes=64)
 
-        offs_t = sb("offs_t", [P, S // 16], U16)
-        nb_t = sb("nb_t", [P, S // 16], U16)
-        pk_t = sb("pk_t", [P, V // 16], U16)
-        cell_t = sb("cell_t", [P, Z // 16], U16)
-        xw_tab = sb("xw_tab", [P, T], U32)
-        xs_tab = sb("xs_tab", [P, T], U8)
-        ew_tab = sb("ew_tab", [P, W], U32)
-        es_tab = sb("es_tab", [P, W], U8)
-        lat_tab = sb("lat_tab", [P, W], F32)
+        def pair(name, shape, dtype=F32):
+            return [sb(f"{name}{h}", shape, dtype) for h in range(2)]
+
+        def half(h, width):
+            return slice(h * width // 2, (h + 1) * width // 2)
+
+        offs_t = sb("offs_t", [P, S // LIST_COLUMN], U16)
+        nb_t = sb("nb_t", [P, S // LIST_COLUMN], U16)
+        pk_t = sb("pk_t", [P, V // LIST_COLUMN], U16)
+        cell_t = sb("cell_t", [P, Z // LIST_COLUMN], U16)
+        x_word_table = sb("x_word_table", [P, T], U32)
+        x_scale_table = sb("x_scale_table", [P, T], U8)
+        e_word_table = sb("e_word_table", [P, W], U32)
+        e_scale_table = sb("e_scale_table", [P, W], U8)
+        lat_table = sb("lat_table", [P, W], F32)
         w_raw = sb("w_raw", [P, PACK, H], F32)
         sc_t = sb("sc_t", [P, PACK, V], F32)
         unit_t = sb("unit_t", [P, PACK], F32)
         y = [sb(f"y{t}", [P, Y_WINDOW], F32) for t in range(PACK)]
+        unread = sb("unread", [P, 2], F32)
+
+        nc.gpsimd.memset(x_scale_table[:].bitcast(I32), 0)
+        nc.gpsimd.memset(y[0][:, S:], 0.0)
+        nc.gpsimd.memset(e_scale_table[:].bitcast(I32), 0)
+        for t in range(1, PACK):
+            nc.gpsimd.memset(y[t][:, S:], 0.0)
 
         def load_scales(queues, table, rows):
             for q, queue in enumerate(queues):
@@ -52,174 +67,138 @@ def tile_picked_ygeolok_dev_p_kernel(tc, x_words, x_scales, w1, sc_, e_words, e_
         def load_words(table, words):
             nc.sync.dma_start(out=table[:].bitcast(I32), in_=words[0].rearrange("p n t -> p (n t)").bitcast(I32))
 
-        nc.gpsimd.memset(xs_tab[:].bitcast(I32), 0)
-        warm = sb("warm", [P, 3], F32)
-        nc.gpsimd.memset(warm[:, 0:1], 0.0)
-        nc.gpsimd.memset(es_tab[:].bitcast(I32), 0)
-        for t in range(PACK):
-            nc.gpsimd.memset(y[t][:, S:], 0.0)
-
         nc.sync.dma_start(out=w_raw[:], in_=w1.rearrange("(p j) c -> p j c", j=PACK))
         nc.sync.dma_start(offs_t[:], offs)
-        load_scales((nc.scalar, nc.scalar, nc.sync, nc.sync), xs_tab, x_scales)
-        nc.scalar.activation(warm[:, 1:2], warm[:, 0:1], ACT.Gelu_apprx_tanh)
-        load_words(xw_tab, x_words)
+        load_scales((nc.scalar, nc.scalar, nc.sync, nc.sync), x_scale_table, x_scales)
+        nc.scalar.activation(unread[:, 0:1], y[0][:, S : S + 1], ACT.Gelu_apprx_tanh)
+        load_words(x_word_table, x_words)
         nc.sync.dma_start(cell_t[:], cell)
-        load_scales((nc.sync,) * 4, es_tab, e_scales)
+        load_scales((nc.sync,) * 4, e_scale_table, e_scales)
         nc.sync.dma_start(nb_t[:], nb)
         nc.sync.dma_start(out=sc_t[:], in_=sc_.rearrange("(p t) v -> p t v", t=PACK))
         nc.sync.dma_start(out=unit_t[:], in_=unit.rearrange("(p t) o -> p (t o)", t=PACK))
-        load_words(ew_tab, e_words)
+        load_words(e_word_table, e_words)
         nc.sync.dma_start(pk_t[:], pk)
-        nc.sync.dma_start(out=lat_tab[:], in_=lat)
+        nc.sync.dma_start(out=lat_table[:], in_=lat)
 
         w_bf = sb("w_bf", [P, PACK, P, PACK], BF16)
         w_dst = w_bf[:].rearrange("p t m j -> p m j t")
         w_src = w_raw[:].rearrange("p j (m t) -> p m j t", t=PACK)
-        xs = sb("xs", [P, S], U8)
-        xw = sb("xw", [P, S], U32)
-        es_b = sb("es_b", [P, Z], U8, tag="w_bf")
-        nc.scalar.copy(w_dst[:, :W_SPLIT], w_src[:, :W_SPLIT])
-        nc.vector.tensor_copy(w_dst[:, W_SPLIT:], w_src[:, W_SPLIT:])
-        nc.vector.tensor_copy(xs[:], xs_tab[:].indirect(offs_t[:]))
-        w_codes = [sb(f"w_codes{u}", [P, H // 2], U32, tag=tag) for u, tag in enumerate(("xs_tab", "xw_tab"))]
-        w_scales = [sb(f"w_scales{u}", [P, H // 2], U8) for u in range(2)]
+        nc.scalar.copy(w_dst[:, :W_GROUPS_ON_SCALAR], w_src[:, :W_GROUPS_ON_SCALAR])
+        nc.vector.tensor_copy(w_dst[:, W_GROUPS_ON_SCALAR:], w_src[:, W_GROUPS_ON_SCALAR:])
+
+        x_scale = sb("x_scale", [P, S], U8)
+        x_word = sb("x_word", [P, S], U32)
+        nc.vector.tensor_copy(x_scale[:], x_scale_table[:].indirect(offs_t[:]))
+
+        w_code = [sb(f"w_code{u}", [P, H // 2], U32, reuse=table) for u, table in enumerate(("x_scale_table", "x_word_table"))]
+        w_scale = [sb(f"w_scale{u}", [P, H // 2], U8) for u in range(2)]
 
         def quantise_w(u):
-            nc.vector.quantize_mx(out=w_codes[u][:].bitcast(FP8X4), scales=w_scales[u][:], in_=w_bf[:, 2 * u : 2 * u + 2].rearrange("p t m j -> p (t m j)"))
+            nc.vector.quantize_mx(out=w_code[u][:].bitcast(FP8X4), scales=w_scale[u][:],
+                                  in_=w_bf[:, 2 * u : 2 * u + 2].rearrange("p t m j -> p (t m j)"))
 
         quantise_w(0)
         for g in range(2):
-            nc.vector.tensor_copy(xw[:, g * (S // 2) : (g + 1) * (S // 2)], xw_tab[:].indirect(offs_t[:, g * (S // 32) : (g + 1) * (S // 32)]))
+            nc.vector.tensor_copy(x_word[:, half(g, S)], x_word_table[:].indirect(offs_t[:, half(g, S // LIST_COLUMN)]))
         quantise_w(1)
 
-        y_ps = [psum.tile([P, S], F32, name=f"y_ps{t}") for t in range(PACK)]
+        y_bank = [psum.tile([P, S], F32, name=f"y_bank{t}") for t in range(PACK)]
         for u in range(2):
             for g in range(2):
-                patches = slice(g * (S // 2), (g + 1) * (S // 2))
-                for t in (2 * u, 2 * u + 1):
-                    cols = slice((t % 2) * P, (t % 2 + 1) * P)
-                    nc.tensor.matmul_mx(out=y_ps[t][:, patches], lhsT=w_codes[u][:, cols].bitcast(FP8X4), lhsT_scale=w_scales[u][:, cols],
-                                        rhs=xw[:, patches].bitcast(FP8X4), rhs_scale=xs[:, patches], start=True, stop=True)
+                for i in range(2):
+                    nc.tensor.matmul_mx(out=y_bank[2 * u + i][:, half(g, S)],
+                                        lhsT=w_code[u][:, half(i, H // 2)].bitcast(FP8X4), lhsT_scale=w_scale[u][:, half(i, H // 2)],
+                                        rhs=x_word[:, half(g, S)].bitcast(FP8X4), rhs_scale=x_scale[:, half(g, S)], start=True, stop=True)
 
-        factor = [sb(f"factor{h}", [P, P, PACK], F32) for h in range(2)]
+        e_scale = sb("e_scale", [P, Z], U8, reuse="w_bf")
+        nc.vector.tensor_copy(e_scale[:], e_scale_table[:].indirect(cell_t[:]))
 
-        def factors(h):
-            cols = slice(h * P, (h + 1) * P)
-            nc.gpsimd.tensor_tensor(factor[h][:], sc_t[:, :, cols].rearrange("p t v -> p v t"),
-                                    unit_t[:].unsqueeze(1).to_broadcast([P, P, PACK]), ALU.mult)
+        factor = sb("factor", [P, V, PACK], F32, reuse="e_scale_table")
+        nc.gpsimd.tensor_tensor(factor[:], sc_t[:].rearrange("p t v -> p v t"), unit_t[:].unsqueeze(1).to_broadcast([P, V, PACK]), ALU.mult)
 
-        ew = sb("ew", [P, Z], U32, tag="cont3")
         yn = [sb(f"yn{t}", [P, S], F32) for t in range(PACK)]
-        cont = [sb(f"cont{t}", [P, S], F32, tag="sc_t" if t == 2 else None) for t in range(PACK)]
-        cpk = [sb(f"cpk{h}", [P, PACK, P], F32) for h in range(2)]
-        apk = [sb(f"apk{h}", [P, P, PACK], F32) for h in range(2)]
-        hid = [sb(f"hid{h}", [P, P, PACK], BF16) for h in range(2)]
-        h_codes = [sb(f"h_codes{h}", [P, P], U32) for h in range(2)]
-        h_scales = [sb(f"h_scales{h}", [P, P], U8) for h in range(2)]
-        sc_ps = [psum.tile([P, Z], F32, name=f"sc_ps{h}") for h in range(2)]
-        halves = [slice(h * P, (h + 1) * P) for h in range(2)]
-
-        def gather(dst, window, on_vector):
-            if on_vector:
-                nc.vector.tensor_copy(dst, window)
-            else:
-                nc.scalar.activation(dst, window, ACT.Copy)
-
-        def copy_y(t, on_vector):
-            if on_vector:
-                nc.vector.tensor_copy(y[t][:, :S], y_ps[t][:])
-            else:
-                nc.scalar.copy(y[t][:, :S], y_ps[t][:])
-
-        def neighbours(t, on_vector):
-            gather(yn[t][:], y[t][:].indirect(nb_t[:]), on_vector)
-
-        def contrast_on_gpsimd(t):
-            nc.gpsimd.tensor_tensor(cont[t][:], yn[t][:], y[t][:, :S], ALU.add)
-
-        def contrast(t):
-            nc.vector.scalar_tensor_tensor(cont[t][:], yn[t][:], -0.7, y_ps[t][:], ALU.mult, ALU.add)
-
-        def crops(h, t, on_vector):
-            gather(cpk[h][:, t, :], cont[t][:].indirect(pk_t[:, h * (P // 16) : (h + 1) * (P // 16)]), on_vector)
-
-        def rectify(h):
-            nc.scalar.activation(apk[h][:].rearrange("p (c i) t -> p c t i", i=4), cpk[h][:].rearrange("p t (c i) -> p c t i", i=4), ACT.Gelu_apprx_tanh)
-
-        def hidden(h):
-            nc.vector.tensor_tensor(hid[h][:], apk[h][:], factor[h][:], ALU.mult)
-
-        def scores(h):
-            nc.vector.quantize_mx(out=h_codes[h][:].bitcast(FP8X4), scales=h_scales[h][:], in_=hid[h][:].rearrange("p v t -> p (v t)"))
-            nc.tensor.matmul_mx(out=sc_ps[h][:], lhsT=h_codes[h][:].bitcast(FP8X4), lhsT_scale=h_scales[h][:],
-                                rhs=ew[:].bitcast(FP8X4), rhs_scale=es_b[:], start=True, stop=True)
-
-        nc.vector.tensor_copy(es_b[:], es_tab[:].indirect(cell_t[:]))
-        factors(0)
-        factors(1)
-        copy_y(0, False)
-        copy_y(1, False)
-        neighbours(0, True)
-        copy_y(2, False)
-        copy_y(3, False)
-        neighbours(1, True)
+        for t in range(PACK):
+            nc.scalar.copy(y[t][:, :S], y_bank[t][:])
+        for t in (0, 1):
+            nc.vector.tensor_copy(yn[t][:], y[t][:].indirect(nb_t[:]))
         nc.scalar.activation(yn[2][:], y[2][:].indirect(nb_t[:]), ACT.Copy, scale=-0.7)
-        contrast(0)
-        contrast_on_gpsimd(2)
-        contrast(1)
-        neighbours(3, False)
-        crops(0, 0, True)
-        crops(1, 0, True)
-        contrast(3)
-        crops(0, 1, False)
-        crops(1, 1, False)
-        crops(0, 2, False)
-        crops(0, 3, True)
-        crops(1, 2, False)
-        crops(1, 3, True)
-        nc.vector.tensor_copy(ew[:], ew_tab[:].indirect(cell_t[:]))
-        rectify(0)
-        rectify(1)
-        hidden(0)
-        scores(0)
-        hidden(1)
-        scores(1)
+        nc.scalar.activation(yn[3][:], y[3][:].indirect(nb_t[:]), ACT.Copy)
 
+        cont = [sb(f"cont{t}", [P, S], F32, reuse="sc_t" if t == 2 else None) for t in range(PACK)]
+        cont_pk = pair("cont_pk", [P, PACK, P])
 
-        nc.scalar.activation(warm[:, 2:3], apk[1][:, 0, 0:1], ACT.Exp)
-        lat_c = sb("lat_c", [P, Z], F32, tag="hid1")
-        nc.vector.tensor_copy(lat_c[:], lat_tab[:].indirect(cell_t[:]))
+        def contrast_on_vector(t):
+            nc.vector.scalar_tensor_tensor(cont[t][:], yn[t][:], -0.7, y_bank[t][:], ALU.mult, ALU.add)
 
-        def pair(name, width):
-            return [sb(f"{name}{h}", [P, width], F32) for h in range(2)]
+        def picked(h, t):
+            return cont[t][:].indirect(pk_t[:, half(h, V // LIST_COLUMN)])
 
-        th, es, el, d2, q, rec, wgt, res = (pair(n, Z) for n in ("th", "es", "el", "d2", "q", "rec", "wgt", "res"))
-        dl = sb("dl", [P, Z], F32)
-        den, num, rden, rden2 = (pair(n, 1) for n in ("den", "num", "rden", "rden2"))
+        contrast_on_vector(0)
+        contrast_on_vector(1)
+        nc.gpsimd.tensor_tensor(cont[2][:], yn[2][:], y[2][:, :S], ALU.add)
         for h in range(2):
-            nc.scalar.activation(th[h][:], sc_ps[h][:], ACT.Tanh)
-            nc.scalar.activation(es[h][:], th[h][:], ACT.Exp, scale=1.3, accum_out=den[h][:])
+            nc.vector.tensor_copy(cont_pk[h][:, 0, :], picked(h, 0))
+        contrast_on_vector(3)
+        for t in (1, 2):
+            for h in range(2):
+                nc.scalar.activation(cont_pk[h][:, t, :], picked(h, t), ACT.Copy)
+        for h in range(2):
+            nc.vector.tensor_copy(cont_pk[h][:, 3, :], picked(h, 3))
+
+        e_word = sb("e_word", [P, Z], U32, reuse="cont3")
+        nc.vector.tensor_copy(e_word[:], e_word_table[:].indirect(cell_t[:]))
+
+        apk = pair("apk", [P, P, PACK])
+        for h in range(2):
+            nc.scalar.activation(apk[h][:].rearrange("p (c i) t -> p c t i", i=LINE),
+                                 cont_pk[h][:].rearrange("p t (c i) -> p c t i", i=LINE), ACT.Gelu_apprx_tanh)
+        nc.scalar.activation(unread[:, 1:2], apk[1][:, 0, 0:1], ACT.Exp)
+
+        hid = pair("hid", [P, P, PACK], BF16)
+        h_code = pair("h_code", [P, P], U32)
+        h_scale = pair("h_scale", [P, P], U8)
+        score_bank = [psum.tile([P, Z], F32, name=f"score_bank{h}") for h in range(2)]
+        for h in range(2):
+            nc.vector.tensor_tensor(hid[h][:], apk[h][:], factor[:, half(h, V), :], ALU.mult)
+            nc.vector.quantize_mx(out=h_code[h][:].bitcast(FP8X4), scales=h_scale[h][:], in_=hid[h][:].rearrange("p v t -> p (v t)"))
+            nc.tensor.matmul_mx(out=score_bank[h][:], lhsT=h_code[h][:].bitcast(FP8X4), lhsT_scale=h_scale[h][:],
+                                rhs=e_word[:].bitcast(FP8X4), rhs_scale=e_scale[:], start=True, stop=True)
+
+        lat_cell = sb("lat_cell", [P, Z], F32, reuse="hid1")
+        nc.vector.tensor_copy(lat_cell[:], lat_table[:].indirect(cell_t[:]))
+
+        tanh_sc, es, neg_el, weight, square, inverse, result = (
+            pair(name, [P, Z]) for name in ("tanh_sc", "es", "neg_el", "weight", "square", "inverse", "result"))
+        den, negnum, rden, rden2 = (pair(name, [P, 1]) for name in ("den", "negnum", "rden", "rden2"))
+        for h in range(2):
+            nc.scalar.activation(tanh_sc[h][:], score_bank[h][:], ACT.Tanh)
+            nc.scalar.activation(es[h][:], tanh_sc[h][:], ACT.Exp, scale=1.3, accum_out=den[h][:])
 
         def numerator(h):
-            nc.vector.scalar_tensor_tensor(el[h][:], es[h][:], -1.0, lat_c[:], ALU.mult, ALU.mult, accum_out=num[h][:])
+            nc.vector.scalar_tensor_tensor(neg_el[h][:], es[h][:], -1.0, lat_cell[:], ALU.mult, ALU.mult, accum_out=negnum[h][:])
 
+        square_bias = (0.25, 0.0)
+        den_dl = sb("den_dl", [P, Z], F32)
+        dl2 = sb("dl2", [P, Z], F32)
+        den2_dl2 = sb("den2_dl2", [P, Z], F32)
         numerator(0)
         nc.vector.reciprocal(rden[0][:], den[0][:])
         numerator(1)
-        nc.vector.tensor_scalar(dl[:], lat_c[:], den[0][:], num[0][:], ALU.mult, ALU.add)
+        nc.vector.tensor_scalar(den_dl[:], lat_cell[:], den[0][:], negnum[0][:], ALU.mult, ALU.add)
         nc.vector.tensor_tensor(rden2[0][:], rden[0][:], rden[0][:], ALU.mult)
-        nc.vector.scalar_tensor_tensor(d2[0][:], dl[:], rden2[0][:], dl[:], ALU.mult, ALU.mult)
+        nc.vector.scalar_tensor_tensor(dl2[:], den_dl[:], rden2[0][:], den_dl[:], ALU.mult, ALU.mult)
         nc.scalar.activation(rden[1][:], den[1][:], ACT.Abs_reciprocal_sqrt, scale=den[1][:])
-        nc.scalar.activation(d2[1][:], lat_c[:], ACT.Square, scale=den[1][:], bias=num[1][:])
+        nc.scalar.activation(den2_dl2[:], lat_cell[:], ACT.Square, scale=den[1][:], bias=negnum[1][:])
         nc.vector.tensor_tensor(rden2[1][:], rden[1][:], rden[1][:], ALU.mult)
-        nc.vector.scalar_tensor_tensor(q[0][:], d2[0][:], 1.0, d2[0][:], ALU.add, ALU.mult)
-        nc.scalar.activation(q[1][:], d2[1][:], ACT.Square, scale=rden2[1][:], bias=0.5)
-        nc.gpsimd.tensor_tensor(wgt[0][:], d2[0][:], es[0][:], ALU.mult)
-        nc.vector.scalar_tensor_tensor(wgt[1][:], d2[1][:], rden2[1][:], es[1][:], ALU.mult, ALU.mult)
-        cells = [slice(0, Z // 2), slice(Z // 2, Z)]
-        for h, bias in enumerate((0.25, 0.0)):
-            for c in cells:
-                nc.scalar.activation(rec[h][:, c], q[h][:, c], ACT.Abs_reciprocal_sqrt, bias=bias)
-                nc.vector.tensor_tensor(res[h][:, c], wgt[h][:, c], rec[h][:, c], ALU.mult)
-                nc.sync.dma_start(out=out[halves[h], c], in_=res[h][:, c])
+        nc.vector.scalar_tensor_tensor(square[0][:], dl2[:], 1.0, dl2[:], ALU.add, ALU.mult)
+        nc.scalar.activation(square[1][:], den2_dl2[:], ACT.Square, scale=rden2[1][:], bias=0.5)
+        nc.vector.tensor_tensor(weight[0][:], dl2[:], es[0][:], ALU.mult)
+        nc.vector.scalar_tensor_tensor(weight[1][:], den2_dl2[:], rden2[1][:], es[1][:], ALU.mult, ALU.mult)
+
+        for h in range(2):
+            for c in range(2):
+                cells = half(c, Z)
+                nc.scalar.activation(inverse[h][:, cells], square[h][:, cells], ACT.Abs_reciprocal_sqrt, bias=square_bias[h])
+                nc.vector.tensor_tensor(result[h][:, cells], weight[h][:, cells], inverse[h][:, cells], ALU.mult)
+                nc.sync.dma_start(out=out[half(h, V), cells], in_=result[h][:, cells])

from contextlib import ExitStack

import concourse.mybir as mybir

K, T, S, H, V, Z, W = 512, 2048, 512, 512, 256, 512, 2048
FLOPS = 2 * K * H * S + 2 * H * V * Z

F32 = mybir.dt.float32
BF16 = mybir.dt.bfloat16
I32 = mybir.dt.int32
U32 = mybir.dt.uint32
U16 = mybir.dt.uint16
U8 = mybir.dt.uint8
FP8X4 = mybir.dt.float8_e4m3fn_x4
ALU = mybir.AluOpType
ACT = mybir.ActivationFunctionType

P = 128
PACK = 4
QUAD = 32
LIST_COLUMN = 16
LINE = 4
Y_WINDOW = 704
W_GROUPS_ON_SCALAR = 80


def tile_picked_ygeolok_dev_p_kernel(tc, x_words, x_scales, w1, sc_, e_words, e_scales, unit, lat, offs, nb, pk, cell, out):
    nc = tc.nc
    with ExitStack() as ctx:
        keep = ctx.enter_context(tc.tile_pool(name="keep", bufs=1))
        psum = ctx.enter_context(tc.psum_pool(name="psum", bufs=1))

        def sb(name, shape, dtype, reuse=None):
            return keep.tile(shape, dtype, name=name, tag=reuse or name, align_bytes=64)

        def pair(name, shape, dtype=F32):
            return [sb(f"{name}{h}", shape, dtype) for h in range(2)]

        def half(h, width):
            return slice(h * width // 2, (h + 1) * width // 2)

        offs_t = sb("offs_t", [P, S // LIST_COLUMN], U16)
        nb_t = sb("nb_t", [P, S // LIST_COLUMN], U16)
        pk_t = sb("pk_t", [P, V // LIST_COLUMN], U16)
        cell_t = sb("cell_t", [P, Z // LIST_COLUMN], U16)
        x_word_table = sb("x_word_table", [P, T], U32)
        x_scale_table = sb("x_scale_table", [P, T], U8)
        e_word_table = sb("e_word_table", [P, W], U32)
        e_scale_table = sb("e_scale_table", [P, W], U8)
        lat_table = sb("lat_table", [P, W], F32)
        w_raw = sb("w_raw", [P, PACK, H], F32)
        sc_t = sb("sc_t", [P, PACK, V], F32)
        unit_t = sb("unit_t", [P, PACK], F32)
        y = [sb(f"y{t}", [P, Y_WINDOW], F32) for t in range(PACK)]
        unread = sb("unread", [P, 2], F32)

        nc.gpsimd.memset(x_scale_table[:].bitcast(I32), 0)
        nc.gpsimd.memset(y[0][:, S:], 0.0)
        nc.gpsimd.memset(e_scale_table[:].bitcast(I32), 0)
        for t in range(1, PACK):
            nc.gpsimd.memset(y[t][:, S:], 0.0)

        def load_scales(queues, table, rows):
            for q, queue in enumerate(queues):
                queue.dma_start(out=table[QUAD * q : QUAD * q + 4, :].bitcast(I32), in_=rows[0, 4 * q : 4 * q + 4, :].bitcast(I32))

        def load_words(table, words):
            nc.sync.dma_start(out=table[:].bitcast(I32), in_=words[0].rearrange("p n t -> p (n t)").bitcast(I32))

        nc.sync.dma_start(out=w_raw[:], in_=w1.rearrange("(p j) c -> p j c", j=PACK))
        nc.sync.dma_start(offs_t[:], offs)
        load_scales((nc.scalar, nc.scalar, nc.sync, nc.sync), x_scale_table, x_scales)
        nc.scalar.activation(unread[:, 0:1], y[0][:, S : S + 1], ACT.Gelu_apprx_tanh)
        load_words(x_word_table, x_words)
        nc.sync.dma_start(cell_t[:], cell)
        load_scales((nc.sync,) * 4, e_scale_table, e_scales)
        nc.sync.dma_start(nb_t[:], nb)
        nc.sync.dma_start(out=sc_t[:], in_=sc_.rearrange("(p t) v -> p t v", t=PACK))
        nc.sync.dma_start(out=unit_t[:], in_=unit.rearrange("(p t) o -> p (t o)", t=PACK))
        load_words(e_word_table, e_words)
        nc.sync.dma_start(pk_t[:], pk)
        nc.sync.dma_start(out=lat_table[:], in_=lat)

        w_bf = sb("w_bf", [P, PACK, P, PACK], BF16)
        w_dst = w_bf[:].rearrange("p t m j -> p m j t")
        w_src = w_raw[:].rearrange("p j (m t) -> p m j t", t=PACK)
        nc.scalar.copy(w_dst[:, :W_GROUPS_ON_SCALAR], w_src[:, :W_GROUPS_ON_SCALAR])
        nc.vector.tensor_copy(w_dst[:, W_GROUPS_ON_SCALAR:], w_src[:, W_GROUPS_ON_SCALAR:])

        x_scale = sb("x_scale", [P, S], U8)
        x_word = sb("x_word", [P, S], U32)
        nc.vector.tensor_copy(x_scale[:], x_scale_table[:].indirect(offs_t[:]))

        w_code = [sb(f"w_code{u}", [P, H // 2], U32, reuse=table) for u, table in enumerate(("x_scale_table", "x_word_table"))]
        w_scale = [sb(f"w_scale{u}", [P, H // 2], U8) for u in range(2)]

        def quantise_w(u):
            nc.vector.quantize_mx(out=w_code[u][:].bitcast(FP8X4), scales=w_scale[u][:],
                                  in_=w_bf[:, 2 * u : 2 * u + 2].rearrange("p t m j -> p (t m j)"))

        quantise_w(0)
        for g in range(2):
            nc.vector.tensor_copy(x_word[:, half(g, S)], x_word_table[:].indirect(offs_t[:, half(g, S // LIST_COLUMN)]))
        quantise_w(1)

        y_bank = [psum.tile([P, S], F32, name=f"y_bank{t}") for t in range(PACK)]
        for u in range(2):
            for g in range(2):
                for i in range(2):
                    nc.tensor.matmul_mx(out=y_bank[2 * u + i][:, half(g, S)],
                                        lhsT=w_code[u][:, half(i, H // 2)].bitcast(FP8X4), lhsT_scale=w_scale[u][:, half(i, H // 2)],
                                        rhs=x_word[:, half(g, S)].bitcast(FP8X4), rhs_scale=x_scale[:, half(g, S)], start=True, stop=True)

        e_scale = sb("e_scale", [P, Z], U8, reuse="w_bf")
        nc.vector.tensor_copy(e_scale[:], e_scale_table[:].indirect(cell_t[:]))

        factor = sb("factor", [P, V, PACK], F32, reuse="e_scale_table")
        nc.gpsimd.tensor_tensor(factor[:], sc_t[:].rearrange("p t v -> p v t"), unit_t[:].unsqueeze(1).to_broadcast([P, V, PACK]), ALU.mult)

        yn = [sb(f"yn{t}", [P, S], F32) for t in range(PACK)]
        for t in range(PACK):
            nc.scalar.copy(y[t][:, :S], y_bank[t][:])
        for t in (0, 1):
            nc.vector.tensor_copy(yn[t][:], y[t][:].indirect(nb_t[:]))
        nc.scalar.activation(yn[2][:], y[2][:].indirect(nb_t[:]), ACT.Copy, scale=-0.7)
        nc.scalar.activation(yn[3][:], y[3][:].indirect(nb_t[:]), ACT.Copy)

        cont = [sb(f"cont{t}", [P, S], F32, reuse="sc_t" if t == 2 else None) for t in range(PACK)]
        cont_pk = pair("cont_pk", [P, PACK, P])

        def contrast_on_vector(t):
            nc.vector.scalar_tensor_tensor(cont[t][:], yn[t][:], -0.7, y_bank[t][:], ALU.mult, ALU.add)

        def picked(h, t):
            return cont[t][:].indirect(pk_t[:, half(h, V // LIST_COLUMN)])

        contrast_on_vector(0)
        contrast_on_vector(1)
        nc.gpsimd.tensor_tensor(cont[2][:], yn[2][:], y[2][:, :S], ALU.add)
        for h in range(2):
            nc.vector.tensor_copy(cont_pk[h][:, 0, :], picked(h, 0))
        contrast_on_vector(3)
        for t in (1, 2):
            for h in range(2):
                nc.scalar.activation(cont_pk[h][:, t, :], picked(h, t), ACT.Copy)
        for h in range(2):
            nc.vector.tensor_copy(cont_pk[h][:, 3, :], picked(h, 3))

        e_word = sb("e_word", [P, Z], U32, reuse="cont3")
        nc.vector.tensor_copy(e_word[:], e_word_table[:].indirect(cell_t[:]))

        apk = pair("apk", [P, P, PACK])
        for h in range(2):
            nc.scalar.activation(apk[h][:].rearrange("p (c i) t -> p c t i", i=LINE),
                                 cont_pk[h][:].rearrange("p t (c i) -> p c t i", i=LINE), ACT.Gelu_apprx_tanh)
        nc.scalar.activation(unread[:, 1:2], apk[1][:, 0, 0:1], ACT.Exp)

        hid = pair("hid", [P, P, PACK], BF16)
        h_code = pair("h_code", [P, P], U32)
        h_scale = pair("h_scale", [P, P], U8)
        score_bank = [psum.tile([P, Z], F32, name=f"score_bank{h}") for h in range(2)]
        for h in range(2):
            nc.vector.tensor_tensor(hid[h][:], apk[h][:], factor[:, half(h, V), :], ALU.mult)
            nc.vector.quantize_mx(out=h_code[h][:].bitcast(FP8X4), scales=h_scale[h][:], in_=hid[h][:].rearrange("p v t -> p (v t)"))
            nc.tensor.matmul_mx(out=score_bank[h][:], lhsT=h_code[h][:].bitcast(FP8X4), lhsT_scale=h_scale[h][:],
                                rhs=e_word[:].bitcast(FP8X4), rhs_scale=e_scale[:], start=True, stop=True)

        lat_cell = sb("lat_cell", [P, Z], F32, reuse="hid1")
        nc.vector.tensor_copy(lat_cell[:], lat_table[:].indirect(cell_t[:]))

        tanh_sc, es, neg_el, weight, square, inverse, result = (
            pair(name, [P, Z]) for name in ("tanh_sc", "es", "neg_el", "weight", "square", "inverse", "result"))
        den, negnum, rden, rden2 = (pair(name, [P, 1]) for name in ("den", "negnum", "rden", "rden2"))
        for h in range(2):
            nc.scalar.activation(tanh_sc[h][:], score_bank[h][:], ACT.Tanh)
            nc.scalar.activation(es[h][:], tanh_sc[h][:], ACT.Exp, scale=1.3, accum_out=den[h][:])

        def numerator(h):
            nc.vector.scalar_tensor_tensor(neg_el[h][:], es[h][:], -1.0, lat_cell[:], ALU.mult, ALU.mult, accum_out=negnum[h][:])

        square_bias = (0.25, 0.0)
        den_dl = sb("den_dl", [P, Z], F32)
        dl2 = sb("dl2", [P, Z], F32)
        den2_dl2 = sb("den2_dl2", [P, Z], F32)
        numerator(0)
        nc.vector.reciprocal(rden[0][:], den[0][:])
        numerator(1)
        nc.vector.tensor_scalar(den_dl[:], lat_cell[:], den[0][:], negnum[0][:], ALU.mult, ALU.add)
        nc.vector.tensor_tensor(rden2[0][:], rden[0][:], rden[0][:], ALU.mult)
        nc.vector.scalar_tensor_tensor(dl2[:], den_dl[:], rden2[0][:], den_dl[:], ALU.mult, ALU.mult)
        nc.scalar.activation(rden[1][:], den[1][:], ACT.Abs_reciprocal_sqrt, scale=den[1][:])
        nc.scalar.activation(den2_dl2[:], lat_cell[:], ACT.Square, scale=den[1][:], bias=negnum[1][:])
        nc.vector.tensor_tensor(rden2[1][:], rden[1][:], rden[1][:], ALU.mult)
        nc.vector.scalar_tensor_tensor(square[0][:], dl2[:], 1.0, dl2[:], ALU.add, ALU.mult)
        nc.scalar.activation(square[1][:], den2_dl2[:], ACT.Square, scale=rden2[1][:], bias=0.5)
        nc.vector.tensor_tensor(weight[0][:], dl2[:], es[0][:], ALU.mult)
        nc.vector.scalar_tensor_tensor(weight[1][:], den2_dl2[:], rden2[1][:], es[1][:], ALU.mult, ALU.mult)

        for h in range(2):
            for c in range(2):
                cells = half(c, Z)
                nc.scalar.activation(inverse[h][:, cells], square[h][:, cells], ACT.Abs_reciprocal_sqrt, bias=square_bias[h])
                nc.vector.tensor_tensor(result[h][:, cells], weight[h][:, cells], inverse[h][:, cells], ALU.mult)
                nc.sync.dma_start(out=out[half(h, V), cells], in_=result[h][:, cells])
